import numpy as np
import ml_dtypes


def mxq(x, axis, fmt="e4m3"):
    dtype, down = {"e4m3": (ml_dtypes.float8_e4m3fn, 7), "e5m2": (ml_dtypes.float8_e5m2, 14)}[fmt]
    v = np.moveaxis(np.asarray(x, np.float32).astype(ml_dtypes.bfloat16).astype(np.float64), axis, -1)
    blocks = v.reshape(v.shape[:-1] + (-1, 32))
    amax = np.abs(blocks).max(-1, keepdims=True)
    byte = np.maximum(np.where(amax > 0, np.frexp(amax)[1] - 1 + 127, 0) - down, 1)
    scale = np.exp2(byte - 127.0)
    codes = (blocks / scale).astype(np.float32).astype(dtype).astype(np.float64)
    return np.moveaxis((codes * scale).reshape(v.shape), -1, axis)


WIDE = False


def mx_kscale(k):
    if not WIDE:
        return np.ones(k)
    levels = np.array([10, -10, 5, -5, 0])
    if k % 512:
        return np.exp2(np.random.permutation(np.resize(levels, k // 32))).repeat(32)
    a = np.empty((k // 512, 16))
    for p in range(k // 512):
        a[p, :8] = np.random.permutation(np.resize(levels, 8))
        for g in range(8):
            far = levels[np.abs(levels - a[p, g]) >= 10]
            a[p, g + 8] = far[np.random.randint(len(far))]
    return np.exp2(a.ravel()).repeat(32)


def f64(x):
    return np.asarray(x).astype(np.float64)


def striped(idx):
    return np.tile(np.asarray(idx).reshape(-1, 16).T, (8, 1)).astype(np.uint16)


def unstriped(offs):
    return offs[:16].T.reshape(-1).astype(np.int64)


E2M1 = np.array([0.0, 0.5, 1.0, 1.5, 2.0, 3.0, 4.0, 6.0, -0.0, -0.5, -1.0, -1.5, -2.0, -3.0, -4.0, -6.0])


def pack_weight(w, fmt):
    k, n = w.shape
    w = f64(np.asarray(w, np.float32).astype(ml_dtypes.bfloat16)).reshape(k // 32, 32, n)
    amax = np.abs(w).max(1)
    if fmt == "e4m3":
        byte = np.frexp(amax)[1] - 1 + 127 - 7
    else:
        mant, ex = np.frexp(amax / 6.0)
        byte = np.where(mant > 0.5, ex, ex - 1) + 127
    byte = np.clip(np.where(amax > 0, byte, 1), 1, 254)
    scaled = (w * np.exp2(127.0 - byte)[:, None, :]).reshape(k, n).astype(np.float32)
    by_word = np.ascontiguousarray(scaled.reshape(k // 512, 128, 4, n).transpose(0, 1, 3, 2))
    if fmt == "e4m3":
        words = by_word.astype(ml_dtypes.float8_e4m3fn).view(np.uint8)
    else:
        c = by_word.astype(ml_dtypes.float4_e2m1fn).view(np.uint8) & 0xF
        words = (c[..., 0::2] | (c[..., 1::2] << 4)).reshape(k // 512, 128, 2 * n)
    return np.ascontiguousarray(words), np.ascontiguousarray(byte.astype(np.uint8).reshape(k // 512, 16, n))


def unpack_weight(words, scales, fmt):
    g, _, n = scales.shape
    words = np.ascontiguousarray(words).reshape(g, 128, n, -1)
    if fmt == "e4m3":
        vals = words.view(ml_dtypes.float8_e4m3fn).astype(np.float64)
    else:
        nib = np.empty((g, 128, n, 4), np.uint8)
        nib[..., 0::2] = words & 0xF
        nib[..., 1::2] = words >> 4
        vals = E2M1[nib]
    vals = vals * np.repeat(np.exp2(scales.astype(np.float64) - 127.0), 8, axis=1)[..., None]
    return vals.transpose(0, 1, 3, 2).reshape(g * 512, n)


D, E, T, I, Q, U = 512, 512, 1024, 256, 512, 1024


def setup_inputs():
    n = np.random.standard_normal
    idx = np.random.permutation(T)[:I]
    idx4 = np.random.permutation(U)[:I]
    fd = mx_kscale(D)
    fe = mx_kscale(E)
    fq = mx_kscale(Q)
    keysp = pack_weight(n((D, T)) / fd[:, None], "e2m1")
    valsp = pack_weight(n((E, T)) / fe[:, None], "e2m1")
    return {
        "query": (n((D, Q)) * 0.9 / np.sqrt(D) * fd[:, None]).astype(np.float32),
        "query2": (n((D, Q)) * 0.6 / np.sqrt(D) * fd[:, None]).astype(np.float32),
        "keys_words": keysp[0],
        "keys_scales": keysp[1],
        "gout": (n((E, Q)) * 1 / np.sqrt(E) * fe[:, None]).astype(np.float32),
        "vals_words": valsp[0],
        "vals_scales": valsp[1],
        "size": (np.random.uniform(0.5, 2.0, (1, I))).astype(np.float32),
        "qs": (np.random.uniform(100.0, 400.0, (Q, 1)) * fq[:, None]).astype(np.float32),
        "qrows": (n((Q, D)) / fq[:, None]).astype(np.float32),
        "old": (n((D, U)) * 4.0).astype(np.float32),
        "fade": (np.random.uniform(0.5, 1.0, (1, U))).astype(np.float32),
        "offs": striped(idx),
        "offs4": striped(idx4),
    }


def reference(query, query2, keys_words, keys_scales, gout, vals_words, vals_scales, size, qs, qrows, old, fade, offs, offs4):
    idx = unstriped(offs)
    idx4 = unstriped(offs4)
    keysu = unpack_weight(keys_words, keys_scales, "e2m1")
    valsu = unpack_weight(vals_words, vals_scales, "e2m1")
    queryq = mxq(f64(query), 0, "e4m3")
    keysidxg = keysu[:, idx]
    a = queryq.T @ keysidxg
    query2q = mxq(f64(query2), 0, "e4m3")
    b = query2q.T @ keysidxg
    pa = np.exp(a - np.max(a, axis=1, keepdims=True))
    wa = pa / np.sum(pa, axis=1, keepdims=True)
    pb = np.exp(b - np.max(b, axis=1, keepdims=True))
    wb = pb / np.sum(pb, axis=1, keepdims=True)
    goutq = mxq(f64(gout), 0, "e4m3")
    valsidxg = valsu[:, idx]
    c0 = goutq.T @ valsidxg
    dwa = c0 * f64(size) / (wa + wb) * wb - c0 * f64(size) * wa * wb / np.square(wa + wb)
    dpa = dwa / np.sum(pa, axis=1, keepdims=True) + np.sum(dwa * pa / np.square(np.sum(pa, axis=1, keepdims=True)) * (-1.0), axis=1, keepdims=True)
    da = dpa * pa
    gs = da * f64(qs)
    qrowsq = mxq(f64(qrows), 0, "e4m3")
    gsq = mxq(gs, 0, "e4m3")
    gk = qrowsq.T @ gsq
    gf = np.zeros((D, U))
    gf[:, idx4] = gk
    y = f64(old) * f64(fade) + gf
    return y

@@ -1,0 +1,269 @@
+from contextlib import ExitStack
+
+import concourse.mybir as mybir
+from concourse.masks import make_identity
+
+F32 = mybir.dt.float32
+BF16 = mybir.dt.bfloat16
+I32 = mybir.dt.int32
+U32 = mybir.dt.uint32
+U16 = mybir.dt.uint16
+U8 = mybir.dt.uint8
+FP8X4 = mybir.dt.float8_e4m3fn_x4
+FP4X4 = mybir.dt.float4_e2m1fn_x4
+ALU = mybir.AluOpType
+ACT = mybir.ActivationFunctionType
+AX = mybir.AxisListType
+
+P = 128
+PACK = 4
+D, E, T, I, Q, U = 512, 512, 1024, 256, 512, 1024
+BANK = 512
+ON_TENSOR = 2
+FLOPS = 2 * Q * I * (D + D + E + D)
+
+
+def tile_attend_bagreement_k_kernel(tc, query, query2, keys_words, keys_scales, gout, vals_words, vals_scales,
+                                     size, qs, qrows, old, fade, offs, offs4, out):
+    nc = tc.nc
+    with ExitStack() as ctx:
+        sb = ctx.enter_context(tc.tile_pool(name="sb", bufs=1))
+        ps = ctx.enter_context(tc.psum_pool(name="ps", bufs=1))
+
+        def tile(name, shape, dtype, after=None):
+            return sb.tile(shape, dtype, name=name, tag=after or name, align_bytes=64)
+
+        def bank(n):
+            return ps.tile([P, BANK], F32, name="bank%d" % n)
+
+        slots = sb.tile([P, I // 16], U16, name="slots")
+        places = sb.tile([P, I // 16], U16, name="places")
+        nc.sync.dma_start(slots[:], offs)
+
+        def load_scales(name, scales):
+            plane = tile(name, [P, T], U8)
+            nc.gpsimd.memset(plane[:].bitcast(I32), 0)
+            for quad in range(4):
+                nc.sync.dma_start(plane[32 * quad : 32 * quad + 4, :].bitcast(I32),
+                                  scales[0, 4 * quad : 4 * quad + 4, :].bitcast(I32))
+            return plane
+
+        def load_words(name, words):
+            pool_words = tile(name, [P, T], U16)
+            nc.sync.dma_start(pool_words[:].bitcast(I32), words[0].bitcast(I32))
+            return pool_words
+
+        def load_rows(name, rows):
+            raw = tile(name, [P, PACK, rows.shape[1]], F32)
+            nc.sync.dma_start(raw[:], rows.rearrange("(p t) w -> p t w", t=PACK))
+            return raw
+
+        key_rows = tile("key_rows", [P, T], U8)
+        for quad in range(4):
+            nc.sync.dma_start(key_rows[32 * quad : 32 * quad + 4, :].bitcast(I32),
+                              keys_scales[0, 4 * quad : 4 * quad + 4, :].bitcast(I32))
+        key_words = load_words("key_words", keys_words)
+        qa_raw = load_rows("qa_raw", query)
+        qb_raw = load_rows("qb_raw", query2)
+        key_scales = tile("key_scales", [P, T], U8)
+        nc.gpsimd.memset(key_scales[:].bitcast(I32), 0)
+        for quad in range(4):
+            live = slice(32 * quad, 32 * quad + 4)
+            nc.vector.tensor_copy(key_scales[live, :].bitcast(I32), key_rows[live, :].bitcast(I32))
+        val_words = load_words("val_words", vals_words)
+        val_scales = load_scales("val_scales", vals_scales)
+        gout_raw = load_rows("gout_raw", gout)
+        rows = tile("rows", [P, P], F32)
+        nc.gpsimd.memset(rows[:], 0.0)
+        nc.sync.dma_start(rows[0:8, :], fade.rearrange("o (c p) -> (o c) p", p=P))
+        nc.sync.dma_start(rows[8:10, :], size.rearrange("o (c p) -> (o c) p", p=P))
+        qs_cols = tile("qs_cols", [P, PACK], F32)
+        nc.sync.dma_start(qs_cols[:], qs.rearrange("(p r) o -> p (r o)", r=PACK))
+        nc.sync.dma_start(places[:], offs4)
+        qrows_raw = load_rows("qrows_raw", qrows)
+        old_tiles = []
+        for t in range(D // P):
+            old_t = tile("old%d" % t, [P, U], F32)
+            nc.sync.dma_start(old_t[:], old[P * t : P * (t + 1), :])
+            old_tiles.append(old_t)
+
+        ident = tile("ident", [P, P], F32)
+        make_identity(nc, ident[:])
+        windows = []
+        for t in range(D // P):
+            window = tile("window%d" % t, [P, U], F32)
+            (nc.vector if t < 2 else nc.gpsimd).memset(window[:], 0.0)
+            windows.append(window)
+
+        def gather(name, words, plane, after=(None, None)):
+            picked_words = tile(name + "_words", [P, I], U16, after=after[0])
+            picked_scales = tile(name + "_scales", [P, I], U8, after=after[1])
+            nc.vector.tensor_copy(picked_words[:], words[:].indirect(slots[:]))
+            nc.vector.tensor_copy(picked_scales[:], plane[:].indirect(slots[:]))
+            return picked_words, picked_scales
+
+        def copy_on(engine, dst, src):
+            if engine == "vector":
+                nc.vector.tensor_copy(dst, src)
+            else:
+                nc.scalar.activation(dst, src, ACT.Copy)
+
+        def quantize(name, grouped, width):
+            codes = tile(name + "_codes", [P, width], U32)
+            scales = tile(name + "_qscales", [P, width], U8)
+            nc.vector.quantize_mx(out=codes[:].bitcast(FP8X4), scales=scales[:], in_=grouped[:])
+            return codes, scales
+
+        def deal_and_quantize(name, raw, on_vector):
+            grouped = tile(name + "_bf", [P, Q * PACK], BF16, after="qa_bf")
+            dst = grouped[:].rearrange("p (r s t) -> p s r t", r=PACK, t=PACK)
+            src = raw[:].rearrange("p t (s r) -> p s r t", r=PACK)
+            if on_vector > 0:
+                copy_on("vector", dst[:, :on_vector], src[:, :on_vector])
+            if on_vector < P:
+                copy_on("scalar", dst[:, on_vector:], src[:, on_vector:])
+            return quantize(name, grouped, Q)
+
+        def scores(stationary, moving, first_bank):
+            banks = [bank(first_bank), bank(first_bank + 1)]
+            for r in range(PACK):
+                nc.tensor.matmul_mx(
+                    out=banks[r // 2][:, I * (r % 2) : I * (r % 2 + 1)],
+                    lhsT=stationary[0][:, P * r : P * (r + 1)].bitcast(FP8X4),
+                    lhsT_scale=stationary[1][:, P * r : P * (r + 1)],
+                    rhs=moving[0][:].bitcast(FP4X4), rhs_scale=moving[1][:], start=True, stop=True)
+            return banks
+
+        def half(banks, r):
+            return banks[r // 2][:, I * (r % 2) : I * (r % 2 + 1)]
+
+        keys = gather("keys", key_words, key_scales)
+        a_banks = scores(deal_and_quantize("qa", qa_raw, 80), keys, 0)
+        neg_a = tile("neg_a", [P, PACK, I], F32)
+        neg_max = tile("neg_max", [P, 2, PACK], F32)
+        sums = tile("sums", [P, 2, PACK], F32)
+        pa = tile("pa", [P, PACK, I], F32)
+        pb = tile("pb", [P, PACK, I], BF16)
+        for r in range(PACK):
+            nc.vector.tensor_scalar(neg_a[:, r, :], half(a_banks, r), -1.0, None, ALU.mult, ALU.min,
+                                    accum_out=neg_max[:, 0, r : r + 1])
+            nc.scalar.activation(pa[:, r, :], neg_a[:, r, :], ACT.Exp, bias=neg_max[:, 0, r : r + 1], scale=-1.0,
+                                 accum_out=sums[:, 0, r : r + 1])
+        b_banks = scores(deal_and_quantize("qb", qb_raw, 64), keys, 2)
+        for h in range(2):
+            nc.vector.tensor_reduce(neg_max[:, 1, 2 * h : 2 * h + 2], b_banks[h][:].rearrange("p (r i) -> p r i", r=2),
+                                    AX.X, ALU.max, negate=True)
+        for r in range(PACK):
+            nc.scalar.activation(pb[:, r, :], half(b_banks, r), ACT.Exp, bias=neg_max[:, 1, r : r + 1],
+                                 accum_out=sums[:, 1, r : r + 1])
+        log_sums = tile("log_sums", [P, 2, PACK], F32)
+        nc.scalar.activation(log_sums[:], sums[:], ACT.Ln)
+        diff = tile("diff", [P, PACK, I], F32)
+        for h in range(2):
+            nc.vector.tensor_tensor(diff[:, 2 * h : 2 * h + 2, :].rearrange("p r i -> p (r i)"), b_banks[h][:],
+                                    neg_a[:, 2 * h : 2 * h + 2, :].rearrange("p r i -> p (r i)"), ALU.add)
+        lse = tile("lse", [P, 2, PACK], F32)
+        nc.vector.tensor_tensor(lse[:], log_sums[:], neg_max[:], ALU.subtract)
+        shift = tile("shift", [P, PACK], F32)
+        nc.vector.tensor_tensor(shift[:], lse[:, 0, :], lse[:, 1, :], ALU.subtract)
+        inv_sum = tile("inv_sum", [P, PACK], F32)
+        nc.vector.reciprocal(inv_sum[:], sums[:, 0, :])
+        row_scale = tile("row_scale", [P, PACK], F32)
+        nc.vector.tensor_tensor(row_scale[:], inv_sum[:], qs_cols[:], ALU.mult)
+
+        turned = bank(0)
+        nc.tensor.transpose(turned[:, :P], rows[:], ident[:])
+        cols = tile("cols", [P, 16], F32)
+        nc.vector.tensor_copy(cols[:], turned[:, :16])
+        size_bank = bank(1)
+        for j in range(4):
+            nc.tensor.transpose(size_bank[:, P * j : P * (j + 1)], cols[:, 8 + j % 2 : 9 + j % 2].to_broadcast([P, P]), ident[:])
+
+        vals = gather("vals", val_words, val_scales, after=("qa_codes", "qa_qscales"))
+        gout_grouped = tile("gout_bf", [P, Q * PACK], BF16, after="qa_bf")
+        dst = gout_grouped[:].rearrange("p (r s t) -> p s r t", r=PACK, t=PACK)
+        src = gout_raw[:].rearrange("p t (s r) -> p s r t", r=PACK)
+        for piece in range(4):
+            part = slice(32 * piece, 32 * (piece + 1))
+            nc.gpsimd.tensor_scalar(dst[:, part], src[:, part], 1.0, 0.0, ALU.mult, ALU.add)
+        c_banks = scores(quantize("gout", gout_grouped, Q), vals, 4)
+        prod = tile("prod", [P, PACK, I], F32)
+        sized = tile("sized", [P, PACK, I], F32)
+        for h in range(2):
+            two = slice(2 * h, 2 * h + 2)
+            nc.vector.tensor_tensor(prod[:, two, :].rearrange("p r i -> p (r i)"), c_banks[h][:],
+                                    pa[:, two, :].rearrange("p r i -> p (r i)"), ALU.mult)
+            nc.vector.tensor_tensor(sized[:, two, :].rearrange("p r i -> p (r i)"), size_bank[:],
+                                    prod[:, two, :].rearrange("p r i -> p (r i)"), ALU.mult)
+
+        share = tile("share", [P, PACK, I], F32)
+        share2 = tile("share2", [P, PACK, I], F32)
+        direct = tile("direct", [P, PACK, I], F32)
+        total = tile("total", [P, PACK], F32)
+        back = tile("back", [P, PACK], F32)
+        gs = tile("gs", [P, PACK, I], BF16)
+        for r in range(PACK):
+            col = slice(r, r + 1)
+            nc.scalar.activation(share[:, r, :], diff[:, r, :], ACT.Sigmoid, bias=shift[:, col])
+            nc.scalar.activation(share2[:, r, :], share[:, r, :], ACT.Square)
+            nc.vector.scalar_tensor_tensor(direct[:, r, :], share2[:, r, :], row_scale[:, col], sized[:, r, :],
+                                           ALU.mult, ALU.mult, accum_out=total[:, col])
+            nc.vector.tensor_scalar(back[:, col], total[:, col], inv_sum[:, col], -1.0, ALU.mult, ALU.mult)
+            nc.vector.scalar_tensor_tensor(gs[:, r, :], pa[:, r, :], back[:, col], direct[:, r, :], ALU.mult, ALU.add)
+        faded_turned = tile("faded_turned", [P, U // P, D], F32, after="diff")
+        for c in range(U // P):
+            turned_old = bank((6, 7, 0, 6, 7, 0, 4, 5)[c])
+            for t in range(D // P):
+                nc.tensor.transpose(turned_old[:, P * t : P * (t + 1)], old_tiles[t][:, P * c : P * (c + 1)], ident[:])
+            nc.scalar.activation(faded_turned[:, c, :], turned_old[:], ACT.Copy, scale=cols[:, c : c + 1])
+
+        gs_grouped = tile("gs_bf", [P, I * PACK], BF16)
+        nc.vector.tensor_copy(gs_grouped[:].rearrange("p (c i r) -> p c r i", i=4, r=PACK),
+                              gs[:].rearrange("p r (c i) -> p c r i", i=4))
+        gs_codes, gs_scales = quantize("gs", gs_grouped, I)
+
+        qrows_grouped = tile("qrows_bf", [P, D * PACK], BF16, after="qa_bf")
+        dst = qrows_grouped[:].rearrange("p (c i t) -> p c t i", i=4, t=PACK)
+        src = qrows_raw[:].rearrange("p t (c i) -> p c t i", i=4)
+        for piece in range(4):
+            part = slice(32 * piece, 32 * (piece + 1))
+            nc.gpsimd.tensor_scalar(dst[:, part], src[:, part], 1.0, 0.0, ALU.mult, ALU.add)
+        qrows_codes, qrows_scales = quantize("qrows", qrows_grouped, D)
+
+        gk_banks = [bank(6), bank(7)]
+        gk = []
+        for t in range(D // P):
+            nc.tensor.matmul_mx(out=half(gk_banks, t), lhsT=qrows_codes[:, P * t : P * (t + 1)].bitcast(FP8X4),
+                                lhsT_scale=qrows_scales[:, P * t : P * (t + 1)],
+                                rhs=gs_codes[:].bitcast(FP8X4), rhs_scale=gs_scales[:], start=True, stop=True)
+        for t in range(D // P):
+            gk_t = tile("gk%d" % t, [P, I], F32)
+            nc.scalar.copy(gk_t[:], half(gk_banks, t))
+            gk.append(gk_t)
+
+        for t in range(D // P):
+            nc.vector.tensor_copy(windows[t][:].indirect(places[:]), gk[t][:])
+            rows_t = slice(P * t, P * (t + 1))
+            for h in range(2):
+                result = tile("result%d_%d" % (t, h), [P, BANK], F32)
+                if t < ON_TENSOR:
+                    window_bank = bank(2 + h)
+                    for j in range(4):
+                        c = 4 * h + j
+                        nc.tensor.transpose(window_bank[:, P * j : P * (j + 1)], windows[t][:, P * c : P * (c + 1)], ident[:])
+                    window_turned = tile("window_turned%d_%d" % (t, h), [P, BANK], F32)
+                    nc.scalar.copy(window_turned[:], window_bank[:])
+                    summed = bank(h)
+                    for j in range(4):
+                        block = slice(P * j, P * (j + 1))
+                        nc.tensor.matmul(summed[:, block], faded_turned[:, 4 * h + j, rows_t], ident[:],
+                                         is_transpose=True, start=True, stop=False)
+                        nc.tensor.matmul(summed[:, block], window_turned[:, block], ident[:],
+                                         is_transpose=True, start=False, stop=True)
+                    nc.scalar.copy(result[:], summed[:])
+                else:
+                    faded = bank((6, 4)[t % 2] + h)
+                    for j in range(4):
+                        nc.tensor.transpose(faded[:, P * j : P * (j + 1)], faded_turned[:, 4 * h + j, rows_t], ident[:])
+                    nc.vector.tensor_tensor(result[:], faded[:], windows[t][:, BANK * h : BANK * (h + 1)], ALU.add)
+                nc.sync.dma_start(out[rows_t, BANK * h : BANK * (h + 1)], result[:])

@@ -19,7 +19,7 @@ P = 128
 PACK = 4
 D, E, T, I, Q, U = 512, 512, 1024, 256, 512, 1024
 BANK = 512
-ON_TENSOR = 2
+ON_TENSOR = 1
 FLOPS = 2 * Q * I * (D + D + E + D)
 
 
@@ -90,9 +90,9 @@ def tile_attend_bagreement_k_kernel(tc, query, query2, keys_words, keys_scales, 
         ident = tile("ident", [P, P], F32)
         make_identity(nc, ident[:])
         windows = []
-        for t in range(D // P):
+        for t in range(3):
             window = tile("window%d" % t, [P, U], F32)
-            (nc.vector if t < 2 else nc.gpsimd).memset(window[:], 0.0)
+            nc.vector.memset(window[:], 0.0)
             windows.append(window)
 
         def gather(name, words, plane, after=(None, None)):
@@ -108,14 +108,14 @@ def tile_attend_bagreement_k_kernel(tc, query, query2, keys_words, keys_scales, 
             else:
                 nc.scalar.activation(dst, src, ACT.Copy)
 
-        def quantize(name, grouped, width):
-            codes = tile(name + "_codes", [P, width], U32)
+        def quantize(name, grouped, width, after=None):
+            codes = tile(name + "_codes", [P, width], U32, after=after)
             scales = tile(name + "_qscales", [P, width], U8)
             nc.vector.quantize_mx(out=codes[:].bitcast(FP8X4), scales=scales[:], in_=grouped[:])
             return codes, scales
 
         def deal_and_quantize(name, raw, on_vector):
-            grouped = tile(name + "_bf", [P, Q * PACK], BF16, after="qa_bf")
+            grouped = tile(name + "_bf", [P, Q * PACK], BF16)
             dst = grouped[:].rearrange("p (r s t) -> p s r t", r=PACK, t=PACK)
             src = raw[:].rearrange("p t (s r) -> p s r t", r=PACK)
             if on_vector > 0:
@@ -149,7 +149,7 @@ def tile_attend_bagreement_k_kernel(tc, query, query2, keys_words, keys_scales, 
                                     accum_out=neg_max[:, 0, r : r + 1])
             nc.scalar.activation(pa[:, r, :], neg_a[:, r, :], ACT.Exp, bias=neg_max[:, 0, r : r + 1], scale=-1.0,
                                  accum_out=sums[:, 0, r : r + 1])
-        b_banks = scores(deal_and_quantize("qb", qb_raw, 64), keys, 2)
+        b_banks = scores(deal_and_quantize("qb", qb_raw, 0), keys, 2)
         for h in range(2):
             nc.vector.tensor_reduce(neg_max[:, 1, 2 * h : 2 * h + 2], b_banks[h][:].rearrange("p (r i) -> p r i", r=2),
                                     AX.X, ALU.max, negate=True)
@@ -158,10 +158,6 @@ def tile_attend_bagreement_k_kernel(tc, query, query2, keys_words, keys_scales, 
                                  accum_out=sums[:, 1, r : r + 1])
         log_sums = tile("log_sums", [P, 2, PACK], F32)
         nc.scalar.activation(log_sums[:], sums[:], ACT.Ln)
-        diff = tile("diff", [P, PACK, I], F32)
-        for h in range(2):
-            nc.vector.tensor_tensor(diff[:, 2 * h : 2 * h + 2, :].rearrange("p r i -> p (r i)"), b_banks[h][:],
-                                    neg_a[:, 2 * h : 2 * h + 2, :].rearrange("p r i -> p (r i)"), ALU.add)
         lse = tile("lse", [P, 2, PACK], F32)
         nc.vector.tensor_tensor(lse[:], log_sums[:], neg_max[:], ALU.subtract)
         shift = tile("shift", [P, PACK], F32)
@@ -180,13 +176,16 @@ def tile_attend_bagreement_k_kernel(tc, query, query2, keys_words, keys_scales, 
             nc.tensor.transpose(size_bank[:, P * j : P * (j + 1)], cols[:, 8 + j % 2 : 9 + j % 2].to_broadcast([P, P]), ident[:])
 
         vals = gather("vals", val_words, val_scales, after=("qa_codes", "qa_qscales"))
-        gout_grouped = tile("gout_bf", [P, Q * PACK], BF16, after="qa_bf")
+        gout_grouped = tile("gout_bf", [P, Q * PACK], BF16, after="qb_bf")
         dst = gout_grouped[:].rearrange("p (r s t) -> p s r t", r=PACK, t=PACK)
         src = gout_raw[:].rearrange("p t (s r) -> p s r t", r=PACK)
-        for piece in range(4):
-            part = slice(32 * piece, 32 * (piece + 1))
-            nc.gpsimd.tensor_scalar(dst[:, part], src[:, part], 1.0, 0.0, ALU.mult, ALU.add)
+        for part in (slice(0, P // 2), slice(P // 2, P)):
+            nc.vector.tensor_copy(dst[:, part], src[:, part])
         c_banks = scores(quantize("gout", gout_grouped, Q), vals, 4)
+        diff = tile("diff", [P, PACK, I], F32, after="qb_bf")
+        for h in range(2):
+            nc.vector.tensor_tensor(diff[:, 2 * h : 2 * h + 2, :].rearrange("p r i -> p (r i)"), b_banks[h][:],
+                                    neg_a[:, 2 * h : 2 * h + 2, :].rearrange("p r i -> p (r i)"), ALU.add)
         prod = tile("prod", [P, PACK, I], F32)
         sized = tile("sized", [P, PACK, I], F32)
         for h in range(2):
@@ -208,27 +207,36 @@ def tile_attend_bagreement_k_kernel(tc, query, query2, keys_words, keys_scales, 
             nc.scalar.activation(share2[:, r, :], share[:, r, :], ACT.Square)
             nc.vector.scalar_tensor_tensor(direct[:, r, :], share2[:, r, :], row_scale[:, col], sized[:, r, :],
                                            ALU.mult, ALU.mult, accum_out=total[:, col])
-            nc.vector.tensor_scalar(back[:, col], total[:, col], inv_sum[:, col], -1.0, ALU.mult, ALU.mult)
-            nc.vector.scalar_tensor_tensor(gs[:, r, :], pa[:, r, :], back[:, col], direct[:, r, :], ALU.mult, ALU.add)
-        faded_turned = tile("faded_turned", [P, U // P, D], F32, after="diff")
-        for c in range(U // P):
-            turned_old = bank((6, 7, 0, 6, 7, 0, 4, 5)[c])
-            for t in range(D // P):
-                nc.tensor.transpose(turned_old[:, P * t : P * (t + 1)], old_tiles[t][:, P * c : P * (c + 1)], ident[:])
-            nc.scalar.activation(faded_turned[:, c, :], turned_old[:], ACT.Copy, scale=cols[:, c : c + 1])
+            if r % 2 == 1:
+                two = slice(r - 1, r + 1)
+                nc.vector.scalar_tensor_tensor(back[:, two], total[:, two], -1.0, inv_sum[:, two], ALU.mult, ALU.mult)
+                for k in (r - 1, r):
+                    nc.vector.scalar_tensor_tensor(gs[:, k, :], pa[:, k, :], back[:, k : k + 1], direct[:, k, :],
+                                                   ALU.mult, ALU.add)
+        qrows_grouped = tile("qrows_bf", [P, D * PACK], BF16, after="share")
+        dst = qrows_grouped[:].rearrange("p (c i t) -> p c t i", i=4, t=PACK)
+        src = qrows_raw[:].rearrange("p t (c i) -> p c t i", i=4)
+        nc.scalar.activation(dst, src, ACT.Copy)
+        def fade_pair(pair, banks, after):
+            turned_pair = tile("faded_turned%d" % pair, [P, U // P, 2 * P], F32, after=after)
+            for two in range(U // P // 2):
+                turned_old = bank(banks[two])
+                for j in range(4):
+                    c, t = 2 * two + j // 2, 2 * pair + j % 2
+                    nc.tensor.transpose(turned_old[:, P * j : P * (j + 1)], old_tiles[t][:, P * c : P * (c + 1)], ident[:])
+                for j in range(2):
+                    c = 2 * two + j
+                    nc.scalar.activation(turned_pair[:, c, :], turned_old[:, 2 * P * j : 2 * P * (j + 1)], ACT.Copy,
+                                         scale=cols[:, c : c + 1])
+            return turned_pair
 
+        faded_turned = [fade_pair(0, (6, 7, 2, 3), "qrows_raw")]
         gs_grouped = tile("gs_bf", [P, I * PACK], BF16)
         nc.vector.tensor_copy(gs_grouped[:].rearrange("p (c i r) -> p c r i", i=4, r=PACK),
                               gs[:].rearrange("p r (c i) -> p c r i", i=4))
         gs_codes, gs_scales = quantize("gs", gs_grouped, I)
 
-        qrows_grouped = tile("qrows_bf", [P, D * PACK], BF16, after="qa_bf")
-        dst = qrows_grouped[:].rearrange("p (c i t) -> p c t i", i=4, t=PACK)
-        src = qrows_raw[:].rearrange("p t (c i) -> p c t i", i=4)
-        for piece in range(4):
-            part = slice(32 * piece, 32 * (piece + 1))
-            nc.gpsimd.tensor_scalar(dst[:, part], src[:, part], 1.0, 0.0, ALU.mult, ALU.add)
-        qrows_codes, qrows_scales = quantize("qrows", qrows_grouped, D)
+        qrows_codes, qrows_scales = quantize("qrows", qrows_grouped, D, after="gs_bf")
 
         gk_banks = [bank(6), bank(7)]
         gk = []
@@ -240,30 +248,33 @@ def tile_attend_bagreement_k_kernel(tc, query, query2, keys_words, keys_scales, 
             gk_t = tile("gk%d" % t, [P, I], F32)
             nc.scalar.copy(gk_t[:], half(gk_banks, t))
             gk.append(gk_t)
+        faded_turned.append(fade_pair(1, (6, 7, 6, 7), None))
 
         for t in range(D // P):
-            nc.vector.tensor_copy(windows[t][:].indirect(places[:]), gk[t][:])
+            window = windows[(0, 1, 2, 1)[t]]
+            nc.vector.tensor_copy(window[:].indirect(places[:]), gk[t][:])
             rows_t = slice(P * t, P * (t + 1))
+            in_pair = slice(P * (t % 2), P * (t % 2 + 1))
             for h in range(2):
                 result = tile("result%d_%d" % (t, h), [P, BANK], F32)
                 if t < ON_TENSOR:
-                    window_bank = bank(2 + h)
+                    window_bank = bank(h)
                     for j in range(4):
                         c = 4 * h + j
-                        nc.tensor.transpose(window_bank[:, P * j : P * (j + 1)], windows[t][:, P * c : P * (c + 1)], ident[:])
-                    window_turned = tile("window_turned%d_%d" % (t, h), [P, BANK], F32)
+                        nc.tensor.transpose(window_bank[:, P * j : P * (j + 1)], window[:, P * c : P * (c + 1)], ident[:])
+                    window_turned = tile("window_turned%d_%d" % (t, h), [P, BANK], F32, after="window_turned%d" % h)
                     nc.scalar.copy(window_turned[:], window_bank[:])
-                    summed = bank(h)
+                    summed = bank(4 + h)
                     for j in range(4):
                         block = slice(P * j, P * (j + 1))
-                        nc.tensor.matmul(summed[:, block], faded_turned[:, 4 * h + j, rows_t], ident[:],
+                        nc.tensor.matmul(summed[:, block], faded_turned[t // 2][:, 4 * h + j, in_pair], ident[:],
                                          is_transpose=True, start=True, stop=False)
                         nc.tensor.matmul(summed[:, block], window_turned[:, block], ident[:],
                                          is_transpose=True, start=False, stop=True)
                     nc.scalar.copy(result[:], summed[:])
                 else:
-                    faded = bank((6, 4)[t % 2] + h)
+                    faded = bank((6, 2)[t % 2] + h)
                     for j in range(4):
-                        nc.tensor.transpose(faded[:, P * j : P * (j + 1)], faded_turned[:, 4 * h + j, rows_t], ident[:])
-                    nc.vector.tensor_tensor(result[:], faded[:], windows[t][:, BANK * h : BANK * (h + 1)], ALU.add)
+                        nc.tensor.transpose(faded[:, P * j : P * (j + 1)], faded_turned[t // 2][:, 4 * h + j, in_pair], ident[:])
+                    nc.vector.tensor_tensor(result[:], faded[:], window[:, BANK * h : BANK * (h + 1)], ALU.add)
                 nc.sync.dma_start(out[rows_t, BANK * h : BANK * (h + 1)], result[:])

@@ -19,7 +19,7 @@ P = 128
 PACK = 4
 D, E, T, I, Q, U = 512, 512, 1024, 256, 512, 1024
 BANK = 512
-ON_TENSOR = 1
+ON_TENSOR = 3
 FLOPS = 2 * Q * I * (D + D + E + D)
 
 
@@ -64,7 +64,12 @@ def tile_attend_bagreement_k_kernel(tc, query, query2, keys_words, keys_scales, 
                               keys_scales[0, 4 * quad : 4 * quad + 4, :].bitcast(I32))
         key_words = load_words("key_words", keys_words)
         qa_raw = load_rows("qa_raw", query)
-        qb_raw = load_rows("qb_raw", query2)
+        qb_raw = [load_rows("qb_raw0", query2[:, : Q // 2])]
+        rows = tile("rows", [P, P], F32)
+        nc.gpsimd.memset(rows[:], 0.0)
+        nc.sync.dma_start(rows[0:8, :], fade.rearrange("o (c p) -> (o c) p", p=P))
+        nc.sync.dma_start(rows[8:10, :], size.rearrange("o (c p) -> (o c) p", p=P))
+        qb_raw.append(load_rows("qb_raw1", query2[:, Q // 2 :]))
         key_scales = tile("key_scales", [P, T], U8)
         nc.gpsimd.memset(key_scales[:].bitcast(I32), 0)
         for quad in range(4):
@@ -72,11 +77,7 @@ def tile_attend_bagreement_k_kernel(tc, query, query2, keys_words, keys_scales, 
             nc.vector.tensor_copy(key_scales[live, :].bitcast(I32), key_rows[live, :].bitcast(I32))
         val_words = load_words("val_words", vals_words)
         val_scales = load_scales("val_scales", vals_scales)
-        gout_raw = load_rows("gout_raw", gout)
-        rows = tile("rows", [P, P], F32)
-        nc.gpsimd.memset(rows[:], 0.0)
-        nc.sync.dma_start(rows[0:8, :], fade.rearrange("o (c p) -> (o c) p", p=P))
-        nc.sync.dma_start(rows[8:10, :], size.rearrange("o (c p) -> (o c) p", p=P))
+        gout_raw = [load_rows("gout_raw%d" % h, gout[:, Q // 2 * h : Q // 2 * (h + 1)]) for h in range(2)]
         qs_cols = tile("qs_cols", [P, PACK], F32)
         nc.sync.dma_start(qs_cols[:], qs.rearrange("(p r) o -> p (r o)", r=PACK))
         nc.sync.dma_start(places[:], offs4)
@@ -121,7 +122,7 @@ def tile_attend_bagreement_k_kernel(tc, query, query2, keys_words, keys_scales, 
             if on_vector > 0:
                 copy_on("vector", dst[:, :on_vector], src[:, :on_vector])
             if on_vector < P:
-                copy_on("scalar", dst[:, on_vector:], src[:, on_vector:])
+                copy_on("scalar", dst[:, on_vector:].rearrange("p s r t -> p s t r"), src[:, on_vector:].rearrange("p s r t -> p s t r"))
             return quantize(name, grouped, Q)
 
         def scores(stationary, moving, first_bank):
@@ -139,17 +140,22 @@ def tile_attend_bagreement_k_kernel(tc, query, query2, keys_words, keys_scales, 
 
         keys = gather("keys", key_words, key_scales)
         a_banks = scores(deal_and_quantize("qa", qa_raw, 80), keys, 0)
-        neg_a = tile("neg_a", [P, PACK, I], F32)
+        qb_grouped = tile("qb_bf", [P, Q * PACK], BF16)
+        dst = qb_grouped[:].rearrange("p (r s t) -> p s t r", r=PACK, t=PACK)
+        for h in range(2):
+            nc.scalar.activation(dst[:, P // 2 * h : P // 2 * (h + 1)],
+                                 qb_raw[h][:].rearrange("p t (s r) -> p s t r", r=PACK), ACT.Copy)
         neg_max = tile("neg_max", [P, 2, PACK], F32)
         sums = tile("sums", [P, 2, PACK], F32)
-        pa = tile("pa", [P, PACK, I], F32)
+        pa = tile("pa", [P, PACK, I], F32, after="qb_raw1")
         pb = tile("pb", [P, PACK, I], BF16)
+        b_banks = scores(quantize("qb", qb_grouped, Q), keys, 2)
+        neg_a = [tile("neg_a0", [P, 2, I], F32), tile("neg_a1", [P, 2, I], F32, after="qb_bf")]
         for r in range(PACK):
-            nc.vector.tensor_scalar(neg_a[:, r, :], half(a_banks, r), -1.0, None, ALU.mult, ALU.min,
+            nc.vector.tensor_scalar(neg_a[r // 2][:, r % 2, :], half(a_banks, r), -1.0, None, ALU.mult, ALU.min,
                                     accum_out=neg_max[:, 0, r : r + 1])
-            nc.scalar.activation(pa[:, r, :], neg_a[:, r, :], ACT.Exp, bias=neg_max[:, 0, r : r + 1], scale=-1.0,
+            nc.scalar.activation(pa[:, r, :], neg_a[r // 2][:, r % 2, :], ACT.Exp, bias=neg_max[:, 0, r : r + 1], scale=-1.0,
                                  accum_out=sums[:, 0, r : r + 1])
-        b_banks = scores(deal_and_quantize("qb", qb_raw, 0), keys, 2)
         for h in range(2):
             nc.vector.tensor_reduce(neg_max[:, 1, 2 * h : 2 * h + 2], b_banks[h][:].rearrange("p (r i) -> p r i", r=2),
                                     AX.X, ALU.max, negate=True)
@@ -158,35 +164,36 @@ def tile_attend_bagreement_k_kernel(tc, query, query2, keys_words, keys_scales, 
                                  accum_out=sums[:, 1, r : r + 1])
         log_sums = tile("log_sums", [P, 2, PACK], F32)
         nc.scalar.activation(log_sums[:], sums[:], ACT.Ln)
-        lse = tile("lse", [P, 2, PACK], F32)
+        turned = bank(6)
+        nc.tensor.transpose(turned[:, :P], rows[:], ident[:])
+        cols = tile("cols", [P, 16], F32)
+        nc.vector.tensor_copy(cols[:], turned[:, :16])
+        size_bank = bank(7)
+        for j in range(4):
+            nc.tensor.transpose(size_bank[:, P * j : P * (j + 1)], cols[:, 8 + j % 2 : 9 + j % 2].to_broadcast([P, P]), ident[:])
+
+        vals = gather("vals", val_words, val_scales, after=("qb_qscales", "keys_scales"))
+        gout_grouped = tile("gout_bf", [P, Q * PACK], BF16, after="qb_codes")
+        dst = gout_grouped[:].rearrange("p (r s t) -> p s r t", r=PACK, t=PACK)
+        for piece in range(4):
+            src = gout_raw[piece // 2][:].rearrange("p t (s r) -> p s r t", r=PACK)
+            nc.gpsimd.tensor_scalar(dst[:, 32 * piece : 32 * (piece + 1)], src[:, 32 * (piece % 2) : 32 * (piece % 2 + 1)],
+                                    1.0, 0.0, ALU.mult, ALU.add)
+        c_banks = scores(quantize("gout", gout_grouped, Q), vals, 4)
+        diff = tile("diff", [P, PACK, I], F32)
+        for h in range(2):
+            nc.vector.tensor_tensor(diff[:, 2 * h : 2 * h + 2, :].rearrange("p r i -> p (r i)"), b_banks[h][:],
+                                    neg_a[h][:].rearrange("p r i -> p (r i)"), ALU.add)
+        lse = tile("lse", [P, 2, PACK], F32, after="gout_qscales")
         nc.vector.tensor_tensor(lse[:], log_sums[:], neg_max[:], ALU.subtract)
         shift = tile("shift", [P, PACK], F32)
         nc.vector.tensor_tensor(shift[:], lse[:, 0, :], lse[:, 1, :], ALU.subtract)
-        inv_sum = tile("inv_sum", [P, PACK], F32)
+        inv_sum = tile("inv_sum", [P, PACK], F32, after="gout_codes")
         nc.vector.reciprocal(inv_sum[:], sums[:, 0, :])
         row_scale = tile("row_scale", [P, PACK], F32)
         nc.vector.tensor_tensor(row_scale[:], inv_sum[:], qs_cols[:], ALU.mult)
 
-        turned = bank(0)
-        nc.tensor.transpose(turned[:, :P], rows[:], ident[:])
-        cols = tile("cols", [P, 16], F32)
-        nc.vector.tensor_copy(cols[:], turned[:, :16])
-        size_bank = bank(1)
-        for j in range(4):
-            nc.tensor.transpose(size_bank[:, P * j : P * (j + 1)], cols[:, 8 + j % 2 : 9 + j % 2].to_broadcast([P, P]), ident[:])
-
-        vals = gather("vals", val_words, val_scales, after=("qa_codes", "qa_qscales"))
-        gout_grouped = tile("gout_bf", [P, Q * PACK], BF16, after="qb_bf")
-        dst = gout_grouped[:].rearrange("p (r s t) -> p s r t", r=PACK, t=PACK)
-        src = gout_raw[:].rearrange("p t (s r) -> p s r t", r=PACK)
-        for part in (slice(0, P // 2), slice(P // 2, P)):
-            nc.vector.tensor_copy(dst[:, part], src[:, part])
-        c_banks = scores(quantize("gout", gout_grouped, Q), vals, 4)
-        diff = tile("diff", [P, PACK, I], F32, after="qb_bf")
-        for h in range(2):
-            nc.vector.tensor_tensor(diff[:, 2 * h : 2 * h + 2, :].rearrange("p r i -> p (r i)"), b_banks[h][:],
-                                    neg_a[:, 2 * h : 2 * h + 2, :].rearrange("p r i -> p (r i)"), ALU.add)
-        prod = tile("prod", [P, PACK, I], F32)
+        prod = tile("prod", [P, PACK, I], F32, after="gout_qscales")
         sized = tile("sized", [P, PACK, I], F32)
         for h in range(2):
             two = slice(2 * h, 2 * h + 2)
@@ -213,51 +220,61 @@ def tile_attend_bagreement_k_kernel(tc, query, query2, keys_words, keys_scales, 
                 for k in (r - 1, r):
                     nc.vector.scalar_tensor_tensor(gs[:, k, :], pa[:, k, :], back[:, k : k + 1], direct[:, k, :],
                                                    ALU.mult, ALU.add)
-        qrows_grouped = tile("qrows_bf", [P, D * PACK], BF16, after="share")
-        dst = qrows_grouped[:].rearrange("p (c i t) -> p c t i", i=4, t=PACK)
-        src = qrows_raw[:].rearrange("p t (c i) -> p c t i", i=4)
-        nc.scalar.activation(dst, src, ACT.Copy)
-        def fade_pair(pair, banks, after):
-            turned_pair = tile("faded_turned%d" % pair, [P, U // P, 2 * P], F32, after=after)
-            for two in range(U // P // 2):
-                turned_old = bank(banks[two])
-                for j in range(4):
-                    c, t = 2 * two + j // 2, 2 * pair + j % 2
-                    nc.tensor.transpose(turned_old[:, P * j : P * (j + 1)], old_tiles[t][:, P * c : P * (c + 1)], ident[:])
-                for j in range(2):
-                    c = 2 * two + j
-                    nc.scalar.activation(turned_pair[:, c, :], turned_old[:, 2 * P * j : 2 * P * (j + 1)], ACT.Copy,
-                                         scale=cols[:, c : c + 1])
-            return turned_pair
+        qrows_grouped = tile("qrows_bf", [P, D * PACK], BF16, after="qb_codes")
+        dst = qrows_grouped[:].rearrange("p (d t) -> p d t", t=PACK)
+        src = qrows_raw[:].rearrange("p t d -> p d t")
+        for piece in range(4):
+            part = slice(P * piece, P * (piece + 1))
+            nc.gpsimd.tensor_scalar(dst[:, part], src[:, part], 1.0, 0.0, ALU.mult, ALU.add)
+        faded_turned = tile("faded_turned", [P, U // P, D], F32, after="share")
 
-        faded_turned = [fade_pair(0, (6, 7, 2, 3), "qrows_raw")]
-        gs_grouped = tile("gs_bf", [P, I * PACK], BF16)
-        nc.vector.tensor_copy(gs_grouped[:].rearrange("p (c i r) -> p c r i", i=4, r=PACK),
-                              gs[:].rearrange("p r (c i) -> p c r i", i=4))
-        gs_codes, gs_scales = quantize("gs", gs_grouped, I)
+        def fade_chunk(c, turned_old):
+            for t in range(D // P):
+                nc.tensor.transpose(turned_old[:, P * t : P * (t + 1)], old_tiles[t][:, P * c : P * (c + 1)], ident[:])
+            nc.scalar.activation(faded_turned[:, c, :], turned_old[:], ACT.Copy, scale=cols[:, c : c + 1])
 
-        qrows_codes, qrows_scales = quantize("qrows", qrows_grouped, D, after="gs_bf")
+        for c in range(6):
+            fade_chunk(c, bank((6, 7, 2, 3)[c % 4]))
+        qrows_codes, qrows_scales = quantize("qrows", qrows_grouped, D, after="gout_qscales")
+        gs_codes = tile("gs_codes", [P, I], U32)
+        gs_scales = tile("gs_scales", [P, I], U8)
+        for h in range(2):
+            some = slice(P * h, P * (h + 1))
+            gs_grouped = tile("gs_bf%d" % h, [P, P * PACK], BF16)
+            nc.vector.tensor_copy(gs_grouped[:].rearrange("p (c i r) -> p c r i", i=4, r=PACK),
+                                  gs[:, :, some].rearrange("p r (c i) -> p c r i", i=4))
+            nc.vector.quantize_mx(out=gs_codes[:, some].bitcast(FP8X4), scales=gs_scales[:, some], in_=gs_grouped[:])
 
+        def key_gradient(target, t, some):
+            nc.tensor.matmul_mx(out=target, lhsT=qrows_codes[:, P * t : P * (t + 1)].bitcast(FP8X4),
+                                lhsT_scale=qrows_scales[:, P * t : P * (t + 1)],
+                                rhs=gs_codes[:, some].bitcast(FP8X4), rhs_scale=gs_scales[:, some], start=True, stop=True)
+
+        first_bank = bank(4)
+        key_gradient(first_bank[:, :P], 0, slice(0, P))
+        first = tile("gk_first", [P, P], F32)
+        nc.scalar.copy(first[:], first_bank[:, :P])
+        nc.vector.tensor_copy(windows[0][:].indirect(places[:, : P // 16]), first[:])
         gk_banks = [bank(6), bank(7)]
         gk = []
         for t in range(D // P):
-            nc.tensor.matmul_mx(out=half(gk_banks, t), lhsT=qrows_codes[:, P * t : P * (t + 1)].bitcast(FP8X4),
-                                lhsT_scale=qrows_scales[:, P * t : P * (t + 1)],
-                                rhs=gs_codes[:].bitcast(FP8X4), rhs_scale=gs_scales[:], start=True, stop=True)
+            width = P if t == 0 else I
+            key_gradient(half(gk_banks, t)[:, :width], t, slice(I - width, I))
         for t in range(D // P):
-            gk_t = tile("gk%d" % t, [P, I], F32)
-            nc.scalar.copy(gk_t[:], half(gk_banks, t))
+            width = P if t == 0 else I
+            gk_t = tile("gk%d" % t, [P, width], F32)
+            nc.scalar.copy(gk_t[:], half(gk_banks, t)[:, :width])
             gk.append(gk_t)
-        faded_turned.append(fade_pair(1, (6, 7, 6, 7), None))
+        for c in (6, 7):
+            fade_chunk(c, bank(c))
 
         for t in range(D // P):
-            window = windows[(0, 1, 2, 1)[t]]
-            nc.vector.tensor_copy(window[:].indirect(places[:]), gk[t][:])
+            window = windows[(0, 1, 2, 2)[t]]
+            nc.vector.tensor_copy(window[:].indirect(places[:, P // 16 :] if t == 0 else places[:]), gk[t][:])
             rows_t = slice(P * t, P * (t + 1))
-            in_pair = slice(P * (t % 2), P * (t % 2 + 1))
             for h in range(2):
                 result = tile("result%d_%d" % (t, h), [P, BANK], F32)
-                if t < ON_TENSOR:
+                if 2 * t + h < ON_TENSOR:
                     window_bank = bank(h)
                     for j in range(4):
                         c = 4 * h + j
@@ -267,14 +284,14 @@ def tile_attend_bagreement_k_kernel(tc, query, query2, keys_words, keys_scales, 
                     summed = bank(4 + h)
                     for j in range(4):
                         block = slice(P * j, P * (j + 1))
-                        nc.tensor.matmul(summed[:, block], faded_turned[t // 2][:, 4 * h + j, in_pair], ident[:],
+                        nc.tensor.matmul(summed[:, block], faded_turned[:, 4 * h + j, rows_t], ident[:],
                                          is_transpose=True, start=True, stop=False)
                         nc.tensor.matmul(summed[:, block], window_turned[:, block], ident[:],
                                          is_transpose=True, start=False, stop=True)
                     nc.scalar.copy(result[:], summed[:])
                 else:
-                    faded = bank((6, 2)[t % 2] + h)
+                    faded = bank((2, 6)[t % 2] + h)
                     for j in range(4):
-                        nc.tensor.transpose(faded[:, P * j : P * (j + 1)], faded_turned[t // 2][:, 4 * h + j, in_pair], ident[:])
+                        nc.tensor.transpose(faded[:, P * j : P * (j + 1)], faded_turned[:, 4 * h + j, rows_t], ident[:])
                     nc.vector.tensor_tensor(result[:], faded[:], window[:, BANK * h : BANK * (h + 1)], ALU.add)
-                nc.sync.dma_start(out[rows_t, BANK * h : BANK * (h + 1)], result[:])
+                (nc.scalar if 2 * t + h < ON_TENSOR else nc.sync).dma_start(out[rows_t, BANK * h : BANK * (h + 1)], result[:])

@@ -19,7 +19,6 @@ P = 128
 PACK = 4
 D, E, T, I, Q, U = 512, 512, 1024, 256, 512, 1024
 BANK = 512
-ON_TENSOR = 3
 FLOPS = 2 * Q * I * (D + D + E + D)
 
 
@@ -122,7 +121,7 @@ def tile_attend_bagreement_k_kernel(tc, query, query2, keys_words, keys_scales, 
             if on_vector > 0:
                 copy_on("vector", dst[:, :on_vector], src[:, :on_vector])
             if on_vector < P:
-                copy_on("scalar", dst[:, on_vector:].rearrange("p s r t -> p s t r"), src[:, on_vector:].rearrange("p s r t -> p s t r"))
+                copy_on("scalar", dst[:, on_vector:], src[:, on_vector:])
             return quantize(name, grouped, Q)
 
         def scores(stationary, moving, first_bank):
@@ -141,14 +140,13 @@ def tile_attend_bagreement_k_kernel(tc, query, query2, keys_words, keys_scales, 
         keys = gather("keys", key_words, key_scales)
         a_banks = scores(deal_and_quantize("qa", qa_raw, 80), keys, 0)
         qb_grouped = tile("qb_bf", [P, Q * PACK], BF16)
-        dst = qb_grouped[:].rearrange("p (r s t) -> p s t r", r=PACK, t=PACK)
+        dst = qb_grouped[:].rearrange("p (r s t) -> p s r t", r=PACK, t=PACK)
         for h in range(2):
             nc.scalar.activation(dst[:, P // 2 * h : P // 2 * (h + 1)],
-                                 qb_raw[h][:].rearrange("p t (s r) -> p s t r", r=PACK), ACT.Copy)
+                                 qb_raw[h][:].rearrange("p t (s r) -> p s r t", r=PACK), ACT.Copy)
         neg_max = tile("neg_max", [P, 2, PACK], F32)
         sums = tile("sums", [P, 2, PACK], F32)
         pa = tile("pa", [P, PACK, I], F32, after="qb_raw1")
-        pb = tile("pb", [P, PACK, I], BF16)
         b_banks = scores(quantize("qb", qb_grouped, Q), keys, 2)
         neg_a = [tile("neg_a0", [P, 2, I], F32), tile("neg_a1", [P, 2, I], F32, after="qb_bf")]
         for r in range(PACK):
@@ -159,6 +157,10 @@ def tile_attend_bagreement_k_kernel(tc, query, query2, keys_words, keys_scales, 
         for h in range(2):
             nc.vector.tensor_reduce(neg_max[:, 1, 2 * h : 2 * h + 2], b_banks[h][:].rearrange("p (r i) -> p r i", r=2),
                                     AX.X, ALU.max, negate=True)
+        gout_grouped = tile("gout_bf", [P, Q * PACK], BF16)
+        gout_dealt = gout_grouped[:].rearrange("p (r s t) -> p s r t", r=PACK, t=PACK)
+        nc.scalar.activation(gout_dealt[:, : P // 2], gout_raw[0][:].rearrange("p t (s r) -> p s r t", r=PACK), ACT.Copy)
+        pb = tile("pb", [P, PACK, I], BF16, after="gout_raw0")
         for r in range(PACK):
             nc.scalar.activation(pb[:, r, :], half(b_banks, r), ACT.Exp, bias=neg_max[:, 1, r : r + 1],
                                  accum_out=sums[:, 1, r : r + 1])
@@ -173,14 +175,9 @@ def tile_attend_bagreement_k_kernel(tc, query, query2, keys_words, keys_scales, 
             nc.tensor.transpose(size_bank[:, P * j : P * (j + 1)], cols[:, 8 + j % 2 : 9 + j % 2].to_broadcast([P, P]), ident[:])
 
         vals = gather("vals", val_words, val_scales, after=("qb_qscales", "keys_scales"))
-        gout_grouped = tile("gout_bf", [P, Q * PACK], BF16, after="qb_codes")
-        dst = gout_grouped[:].rearrange("p (r s t) -> p s r t", r=PACK, t=PACK)
-        for piece in range(4):
-            src = gout_raw[piece // 2][:].rearrange("p t (s r) -> p s r t", r=PACK)
-            nc.gpsimd.tensor_scalar(dst[:, 32 * piece : 32 * (piece + 1)], src[:, 32 * (piece % 2) : 32 * (piece % 2 + 1)],
-                                    1.0, 0.0, ALU.mult, ALU.add)
+        nc.vector.tensor_copy(gout_dealt[:, P // 2 :], gout_raw[1][:].rearrange("p t (s r) -> p s r t", r=PACK))
         c_banks = scores(quantize("gout", gout_grouped, Q), vals, 4)
-        diff = tile("diff", [P, PACK, I], F32)
+        diff = tile("diff", [P, PACK, I], F32, after="gout_raw1")
         for h in range(2):
             nc.vector.tensor_tensor(diff[:, 2 * h : 2 * h + 2, :].rearrange("p r i -> p (r i)"), b_banks[h][:],
                                     neg_a[h][:].rearrange("p r i -> p (r i)"), ALU.add)
@@ -220,22 +217,19 @@ def tile_attend_bagreement_k_kernel(tc, query, query2, keys_words, keys_scales, 
                 for k in (r - 1, r):
                     nc.vector.scalar_tensor_tensor(gs[:, k, :], pa[:, k, :], back[:, k : k + 1], direct[:, k, :],
                                                    ALU.mult, ALU.add)
-        qrows_grouped = tile("qrows_bf", [P, D * PACK], BF16, after="qb_codes")
-        dst = qrows_grouped[:].rearrange("p (d t) -> p d t", t=PACK)
-        src = qrows_raw[:].rearrange("p t d -> p d t")
-        for piece in range(4):
-            part = slice(P * piece, P * (piece + 1))
-            nc.gpsimd.tensor_scalar(dst[:, part], src[:, part], 1.0, 0.0, ALU.mult, ALU.add)
-        faded_turned = tile("faded_turned", [P, U // P, D], F32, after="share")
+        qrows_grouped = tile("qrows_bf", [P, D * PACK], BF16, after="share")
+        nc.scalar.activation(qrows_grouped[:].rearrange("p (c i t) -> p c t i", i=4, t=PACK),
+                             qrows_raw[:].rearrange("p t (c i) -> p c t i", i=4), ACT.Copy)
+        faded_turned = tile("faded_turned", [P, U // P, D], F32, after="qrows_raw")
 
         def fade_chunk(c, turned_old):
             for t in range(D // P):
                 nc.tensor.transpose(turned_old[:, P * t : P * (t + 1)], old_tiles[t][:, P * c : P * (c + 1)], ident[:])
             nc.scalar.activation(faded_turned[:, c, :], turned_old[:], ACT.Copy, scale=cols[:, c : c + 1])
 
-        for c in range(6):
-            fade_chunk(c, bank((6, 7, 2, 3)[c % 4]))
-        qrows_codes, qrows_scales = quantize("qrows", qrows_grouped, D, after="gout_qscales")
+        for c in range(4):
+            fade_chunk(c, bank((2, 3, 6, 7)[c]))
+        qrows_codes, qrows_scales = quantize("qrows", qrows_grouped, D, after="direct")
         gs_codes = tile("gs_codes", [P, I], U32)
         gs_scales = tile("gs_scales", [P, I], U8)
         for h in range(2):
@@ -265,33 +259,17 @@ def tile_attend_bagreement_k_kernel(tc, query, query2, keys_words, keys_scales, 
             gk_t = tile("gk%d" % t, [P, width], F32)
             nc.scalar.copy(gk_t[:], half(gk_banks, t)[:, :width])
             gk.append(gk_t)
-        for c in (6, 7):
-            fade_chunk(c, bank(c))
+        for c in range(4, 8):
+            fade_chunk(c, bank(6 + c % 2))
 
         for t in range(D // P):
-            window = windows[(0, 1, 2, 2)[t]]
+            window = windows[t % 3]
             nc.vector.tensor_copy(window[:].indirect(places[:, P // 16 :] if t == 0 else places[:]), gk[t][:])
             rows_t = slice(P * t, P * (t + 1))
             for h in range(2):
+                faded = bank(2 * (t % 3) + h)
+                for j in range(4):
+                    nc.tensor.transpose(faded[:, P * j : P * (j + 1)], faded_turned[:, 4 * h + j, rows_t], ident[:])
                 result = tile("result%d_%d" % (t, h), [P, BANK], F32)
-                if 2 * t + h < ON_TENSOR:
-                    window_bank = bank(h)
-                    for j in range(4):
-                        c = 4 * h + j
-                        nc.tensor.transpose(window_bank[:, P * j : P * (j + 1)], window[:, P * c : P * (c + 1)], ident[:])
-                    window_turned = tile("window_turned%d_%d" % (t, h), [P, BANK], F32, after="window_turned%d" % h)
-                    nc.scalar.copy(window_turned[:], window_bank[:])
-                    summed = bank(4 + h)
-                    for j in range(4):
-                        block = slice(P * j, P * (j + 1))
-                        nc.tensor.matmul(summed[:, block], faded_turned[:, 4 * h + j, rows_t], ident[:],
-                                         is_transpose=True, start=True, stop=False)
-                        nc.tensor.matmul(summed[:, block], window_turned[:, block], ident[:],
-                                         is_transpose=True, start=False, stop=True)
-                    nc.scalar.copy(result[:], summed[:])
-                else:
-                    faded = bank((2, 6)[t % 2] + h)
-                    for j in range(4):
-                        nc.tensor.transpose(faded[:, P * j : P * (j + 1)], faded_turned[:, 4 * h + j, rows_t], ident[:])
-                    nc.vector.tensor_tensor(result[:], faded[:], window[:, BANK * h : BANK * (h + 1)], ALU.add)
-                (nc.scalar if 2 * t + h < ON_TENSOR else nc.sync).dma_start(out[rows_t, BANK * h : BANK * (h + 1)], result[:])
+                nc.vector.tensor_tensor(result[:], faded[:], window[:, BANK * h : BANK * (h + 1)], ALU.add)
+                nc.sync.dma_start(out[rows_t, BANK * h : BANK * (h + 1)], result[:])

from contextlib import ExitStack

import concourse.mybir as mybir
from concourse.masks import make_identity

F32 = mybir.dt.float32
BF16 = mybir.dt.bfloat16
I32 = mybir.dt.int32
U32 = mybir.dt.uint32
U16 = mybir.dt.uint16
U8 = mybir.dt.uint8
FP8X4 = mybir.dt.float8_e4m3fn_x4
FP4X4 = mybir.dt.float4_e2m1fn_x4
ALU = mybir.AluOpType
ACT = mybir.ActivationFunctionType
AX = mybir.AxisListType

P = 128
PACK = 4
D, E, T, I, Q, U = 512, 512, 1024, 256, 512, 1024
BANK = 512
FLOPS = 2 * Q * I * (D + D + E + D)


def tile_attend_bagreement_k_kernel(tc, query, query2, keys_words, keys_scales, gout, vals_words, vals_scales,
                                     size, qs, qrows, old, fade, offs, offs4, out):
    nc = tc.nc
    with ExitStack() as ctx:
        sb = ctx.enter_context(tc.tile_pool(name="sb", bufs=1))
        ps = ctx.enter_context(tc.psum_pool(name="ps", bufs=1))

        def tile(name, shape, dtype, after=None):
            return sb.tile(shape, dtype, name=name, tag=after or name, align_bytes=64)

        def bank(n):
            return ps.tile([P, BANK], F32, name="bank%d" % n)

        slots = sb.tile([P, I // 16], U16, name="slots")
        places = sb.tile([P, I // 16], U16, name="places")
        nc.sync.dma_start(slots[:], offs)

        def load_scales(name, scales):
            plane = tile(name, [P, T], U8)
            nc.gpsimd.memset(plane[:].bitcast(I32), 0)
            for quad in range(4):
                nc.sync.dma_start(plane[32 * quad : 32 * quad + 4, :].bitcast(I32),
                                  scales[0, 4 * quad : 4 * quad + 4, :].bitcast(I32))
            return plane

        def load_words(name, words):
            pool_words = tile(name, [P, T], U16)
            nc.sync.dma_start(pool_words[:].bitcast(I32), words[0].bitcast(I32))
            return pool_words

        def load_rows(name, rows):
            raw = tile(name, [P, PACK, rows.shape[1]], F32)
            nc.sync.dma_start(raw[:], rows.rearrange("(p t) w -> p t w", t=PACK))
            return raw

        key_rows = tile("key_rows", [P, T], U8)
        for quad in range(4):
            nc.sync.dma_start(key_rows[32 * quad : 32 * quad + 4, :].bitcast(I32),
                              keys_scales[0, 4 * quad : 4 * quad + 4, :].bitcast(I32))
        key_words = load_words("key_words", keys_words)
        qa_raw = load_rows("qa_raw", query)
        qb_raw = [load_rows("qb_raw0", query2[:, : Q // 2])]
        rows = tile("rows", [P, P], F32)
        nc.gpsimd.memset(rows[:], 0.0)
        nc.sync.dma_start(rows[0:8, :], fade.rearrange("o (c p) -> (o c) p", p=P))
        nc.sync.dma_start(rows[8:10, :], size.rearrange("o (c p) -> (o c) p", p=P))
        qb_raw.append(load_rows("qb_raw1", query2[:, Q // 2 :]))
        key_scales = tile("key_scales", [P, T], U8)
        nc.gpsimd.memset(key_scales[:].bitcast(I32), 0)
        for quad in range(4):
            live = slice(32 * quad, 32 * quad + 4)
            nc.vector.tensor_copy(key_scales[live, :].bitcast(I32), key_rows[live, :].bitcast(I32))
        val_words = load_words("val_words", vals_words)
        val_scales = load_scales("val_scales", vals_scales)
        gout_raw = [load_rows("gout_raw%d" % h, gout[:, Q // 2 * h : Q // 2 * (h + 1)]) for h in range(2)]
        qs_cols = tile("qs_cols", [P, PACK], F32)
        nc.sync.dma_start(qs_cols[:], qs.rearrange("(p r) o -> p (r o)", r=PACK))
        nc.sync.dma_start(places[:], offs4)
        qrows_raw = load_rows("qrows_raw", qrows)
        old_tiles = []
        for t in range(D // P):
            old_t = tile("old%d" % t, [P, U], F32)
            nc.sync.dma_start(old_t[:], old[P * t : P * (t + 1), :])
            old_tiles.append(old_t)

        ident = tile("ident", [P, P], F32)
        make_identity(nc, ident[:])
        windows = []
        for t in range(3):
            window = tile("window%d" % t, [P, U], F32)
            nc.vector.memset(window[:], 0.0)
            windows.append(window)

        def gather(name, words, plane, after=(None, None)):
            picked_words = tile(name + "_words", [P, I], U16, after=after[0])
            picked_scales = tile(name + "_scales", [P, I], U8, after=after[1])
            nc.vector.tensor_copy(picked_words[:], words[:].indirect(slots[:]))
            nc.vector.tensor_copy(picked_scales[:], plane[:].indirect(slots[:]))
            return picked_words, picked_scales

        def copy_on(engine, dst, src):
            if engine == "vector":
                nc.vector.tensor_copy(dst, src)
            else:
                nc.scalar.activation(dst, src, ACT.Copy)

        def quantize(name, grouped, width, after=None):
            codes = tile(name + "_codes", [P, width], U32, after=after)
            scales = tile(name + "_qscales", [P, width], U8)
            nc.vector.quantize_mx(out=codes[:].bitcast(FP8X4), scales=scales[:], in_=grouped[:])
            return codes, scales

        def deal_and_quantize(name, raw, on_vector):
            grouped = tile(name + "_bf", [P, Q * PACK], BF16)
            dst = grouped[:].rearrange("p (r s t) -> p s r t", r=PACK, t=PACK)
            src = raw[:].rearrange("p t (s r) -> p s r t", r=PACK)
            if on_vector > 0:
                copy_on("vector", dst[:, :on_vector], src[:, :on_vector])
            if on_vector < P:
                copy_on("scalar", dst[:, on_vector:], src[:, on_vector:])
            return quantize(name, grouped, Q)

        def scores(stationary, moving, first_bank):
            banks = [bank(first_bank), bank(first_bank + 1)]
            for r in range(PACK):
                nc.tensor.matmul_mx(
                    out=banks[r // 2][:, I * (r % 2) : I * (r % 2 + 1)],
                    lhsT=stationary[0][:, P * r : P * (r + 1)].bitcast(FP8X4),
                    lhsT_scale=stationary[1][:, P * r : P * (r + 1)],
                    rhs=moving[0][:].bitcast(FP4X4), rhs_scale=moving[1][:], start=True, stop=True)
            return banks

        def half(banks, r):
            return banks[r // 2][:, I * (r % 2) : I * (r % 2 + 1)]

        keys = gather("keys", key_words, key_scales)
        a_banks = scores(deal_and_quantize("qa", qa_raw, 80), keys, 0)
        qb_grouped = tile("qb_bf", [P, Q * PACK], BF16)
        dst = qb_grouped[:].rearrange("p (r s t) -> p s r t", r=PACK, t=PACK)
        for h in range(2):
            nc.scalar.activation(dst[:, P // 2 * h : P // 2 * (h + 1)],
                                 qb_raw[h][:].rearrange("p t (s r) -> p s r t", r=PACK), ACT.Copy)
        neg_max = tile("neg_max", [P, 2, PACK], F32)
        sums = tile("sums", [P, 2, PACK], F32)
        pa = tile("pa", [P, PACK, I], F32, after="qb_raw1")
        b_banks = scores(quantize("qb", qb_grouped, Q), keys, 2)
        neg_a = [tile("neg_a0", [P, 2, I], F32), tile("neg_a1", [P, 2, I], F32, after="qb_bf")]
        for r in range(PACK):
            nc.vector.tensor_scalar(neg_a[r // 2][:, r % 2, :], half(a_banks, r), -1.0, None, ALU.mult, ALU.min,
                                    accum_out=neg_max[:, 0, r : r + 1])
            nc.scalar.activation(pa[:, r, :], neg_a[r // 2][:, r % 2, :], ACT.Exp, bias=neg_max[:, 0, r : r + 1], scale=-1.0,
                                 accum_out=sums[:, 0, r : r + 1])
        for h in range(2):
            nc.vector.tensor_reduce(neg_max[:, 1, 2 * h : 2 * h + 2], b_banks[h][:].rearrange("p (r i) -> p r i", r=2),
                                    AX.X, ALU.max, negate=True)
        gout_grouped = tile("gout_bf", [P, Q * PACK], BF16)
        gout_dealt = gout_grouped[:].rearrange("p (r s t) -> p s r t", r=PACK, t=PACK)
        nc.scalar.activation(gout_dealt[:, : P // 2], gout_raw[0][:].rearrange("p t (s r) -> p s r t", r=PACK), ACT.Copy)
        pb = tile("pb", [P, PACK, I], BF16, after="gout_raw0")
        for r in range(PACK):
            nc.scalar.activation(pb[:, r, :], half(b_banks, r), ACT.Exp, bias=neg_max[:, 1, r : r + 1],
                                 accum_out=sums[:, 1, r : r + 1])
        log_sums = tile("log_sums", [P, 2, PACK], F32)
        nc.scalar.activation(log_sums[:], sums[:], ACT.Ln)
        turned = bank(6)
        nc.tensor.transpose(turned[:, :P], rows[:], ident[:])
        cols = tile("cols", [P, 16], F32)
        nc.vector.tensor_copy(cols[:], turned[:, :16])
        size_bank = bank(7)
        for j in range(4):
            nc.tensor.transpose(size_bank[:, P * j : P * (j + 1)], cols[:, 8 + j % 2 : 9 + j % 2].to_broadcast([P, P]), ident[:])

        vals = gather("vals", val_words, val_scales, after=("qb_qscales", "keys_scales"))
        nc.vector.tensor_copy(gout_dealt[:, P // 2 :], gout_raw[1][:].rearrange("p t (s r) -> p s r t", r=PACK))
        c_banks = scores(quantize("gout", gout_grouped, Q), vals, 4)
        diff = tile("diff", [P, PACK, I], F32, after="gout_raw1")
        for h in range(2):
            nc.vector.tensor_tensor(diff[:, 2 * h : 2 * h + 2, :].rearrange("p r i -> p (r i)"), b_banks[h][:],
                                    neg_a[h][:].rearrange("p r i -> p (r i)"), ALU.add)
        lse = tile("lse", [P, 2, PACK], F32, after="gout_qscales")
        nc.vector.tensor_tensor(lse[:], log_sums[:], neg_max[:], ALU.subtract)
        shift = tile("shift", [P, PACK], F32)
        nc.vector.tensor_tensor(shift[:], lse[:, 0, :], lse[:, 1, :], ALU.subtract)
        inv_sum = tile("inv_sum", [P, PACK], F32, after="gout_codes")
        nc.vector.reciprocal(inv_sum[:], sums[:, 0, :])
        row_scale = tile("row_scale", [P, PACK], F32)
        nc.vector.tensor_tensor(row_scale[:], inv_sum[:], qs_cols[:], ALU.mult)

        prod = tile("prod", [P, PACK, I], F32, after="gout_qscales")
        sized = tile("sized", [P, PACK, I], F32)
        for h in range(2):
            two = slice(2 * h, 2 * h + 2)
            nc.vector.tensor_tensor(prod[:, two, :].rearrange("p r i -> p (r i)"), c_banks[h][:],
                                    pa[:, two, :].rearrange("p r i -> p (r i)"), ALU.mult)
            nc.vector.tensor_tensor(sized[:, two, :].rearrange("p r i -> p (r i)"), size_bank[:],
                                    prod[:, two, :].rearrange("p r i -> p (r i)"), ALU.mult)

        share = tile("share", [P, PACK, I], F32)
        share2 = tile("share2", [P, PACK, I], F32)
        direct = tile("direct", [P, PACK, I], F32)
        total = tile("total", [P, PACK], F32)
        back = tile("back", [P, PACK], F32)
        gs = tile("gs", [P, PACK, I], BF16)
        for r in range(PACK):
            col = slice(r, r + 1)
            nc.scalar.activation(share[:, r, :], diff[:, r, :], ACT.Sigmoid, bias=shift[:, col])
            nc.scalar.activation(share2[:, r, :], share[:, r, :], ACT.Square)
            nc.vector.scalar_tensor_tensor(direct[:, r, :], share2[:, r, :], row_scale[:, col], sized[:, r, :],
                                           ALU.mult, ALU.mult, accum_out=total[:, col])
            if r % 2 == 1:
                two = slice(r - 1, r + 1)
                nc.vector.scalar_tensor_tensor(back[:, two], total[:, two], -1.0, inv_sum[:, two], ALU.mult, ALU.mult)
                for k in (r - 1, r):
                    nc.vector.scalar_tensor_tensor(gs[:, k, :], pa[:, k, :], back[:, k : k + 1], direct[:, k, :],
                                                   ALU.mult, ALU.add)
        qrows_grouped = tile("qrows_bf", [P, D * PACK], BF16, after="share")
        nc.scalar.activation(qrows_grouped[:].rearrange("p (c i t) -> p c t i", i=4, t=PACK),
                             qrows_raw[:].rearrange("p t (c i) -> p c t i", i=4), ACT.Copy)
        faded_turned = tile("faded_turned", [P, U // P, D], F32, after="qrows_raw")

        def fade_chunk(c, turned_old):
            for t in range(D // P):
                nc.tensor.transpose(turned_old[:, P * t : P * (t + 1)], old_tiles[t][:, P * c : P * (c + 1)], ident[:])
            nc.scalar.activation(faded_turned[:, c, :], turned_old[:], ACT.Copy, scale=cols[:, c : c + 1])

        for c in range(4):
            fade_chunk(c, bank((2, 3, 6, 7)[c]))
        qrows_codes, qrows_scales = quantize("qrows", qrows_grouped, D, after="direct")
        gs_codes = tile("gs_codes", [P, I], U32)
        gs_scales = tile("gs_scales", [P, I], U8)
        for h in range(2):
            some = slice(P * h, P * (h + 1))
            gs_grouped = tile("gs_bf%d" % h, [P, P * PACK], BF16)
            nc.vector.tensor_copy(gs_grouped[:].rearrange("p (c i r) -> p c r i", i=4, r=PACK),
                                  gs[:, :, some].rearrange("p r (c i) -> p c r i", i=4))
            nc.vector.quantize_mx(out=gs_codes[:, some].bitcast(FP8X4), scales=gs_scales[:, some], in_=gs_grouped[:])

        def key_gradient(target, t, some):
            nc.tensor.matmul_mx(out=target, lhsT=qrows_codes[:, P * t : P * (t + 1)].bitcast(FP8X4),
                                lhsT_scale=qrows_scales[:, P * t : P * (t + 1)],
                                rhs=gs_codes[:, some].bitcast(FP8X4), rhs_scale=gs_scales[:, some], start=True, stop=True)

        first_bank = bank(4)
        key_gradient(first_bank[:, :P], 0, slice(0, P))
        first = tile("gk_first", [P, P], F32)
        nc.scalar.copy(first[:], first_bank[:, :P])
        nc.vector.tensor_copy(windows[0][:].indirect(places[:, : P // 16]), first[:])
        gk_banks = [bank(6), bank(7)]
        gk = []
        for t in range(D // P):
            width = P if t == 0 else I
            key_gradient(half(gk_banks, t)[:, :width], t, slice(I - width, I))
        for t in range(D // P):
            width = P if t == 0 else I
            gk_t = tile("gk%d" % t, [P, width], F32)
            nc.scalar.copy(gk_t[:], half(gk_banks, t)[:, :width])
            gk.append(gk_t)
        for c in range(4, 8):
            fade_chunk(c, bank(6 + c % 2))

        for t in range(D // P):
            window = windows[t % 3]
            nc.vector.tensor_copy(window[:].indirect(places[:, P // 16 :] if t == 0 else places[:]), gk[t][:])
            rows_t = slice(P * t, P * (t + 1))
            for h in range(2):
                faded = bank(2 * (t % 3) + h)
                for j in range(4):
                    nc.tensor.transpose(faded[:, P * j : P * (j + 1)], faded_turned[:, 4 * h + j, rows_t], ident[:])
                result = tile("result%d_%d" % (t, h), [P, BANK], F32)
                nc.vector.tensor_tensor(result[:], faded[:], window[:, BANK * h : BANK * (h + 1)], ALU.add)
                nc.sync.dma_start(out[rows_t, BANK * h : BANK * (h + 1)], result[:])
